import numpy as np, ml_dtypes
CORES = [6,15,38,47]
N = 4
BF = ml_dtypes.bfloat16
def gentries(a):
    return np.ascontiguousarray(a.reshape(8, 16, -1).transpose(0, 2, 1)).reshape(8, -1)
def gtable(e):
    e = np.asarray(e); return np.ascontiguousarray(e.reshape(8, -1, 16).transpose(0, 2, 1)).reshape(128, -1).astype(np.int32)
W, K, F, O, C, V = 4096, 640, 2, 4, 8, 250
def pick(a, ix):
    return np.take_along_axis(a, ix[:, None, :], 2)
def draw_lists(rng):
    return rng.permuted(np.tile(np.arange(W, dtype=np.int64), (N, 8, N, F, O, 1)), axis=-1)[..., :K].copy()
def frames(rng, T, L, share):
    o = rng.integers(0, O, (N, 8, N, F)); B = np.zeros((N, 8, 16, N, F, K), np.int64)
    for r in range(N):
        for q in range(N):
            for f in range(F):
                v = pick(T[q], L[r, np.arange(8), q, f, o[r, :, q, f]]) + rng.integers(-10, 11, (8, 16, K))
                m = rng.random((8, 16, K)) < share[r, :, q, f][:, None, None]
                B[r, :, :, q, f] = np.clip(np.where(m, v, rng.integers(-V, V + 1, (8, 16, K))), -V, V)
    return B
def pack(R, B, L):
    return {"ref0": np.ascontiguousarray(R.reshape(N, 128, W)).astype(np.float32).astype(BF), "obs": np.ascontiguousarray(B.reshape(N, 128, N * F * K)).astype(np.float32).astype(BF),
            "ops": np.stack([gtable(a.reshape(8, -1)) for a in L])}
def setup_inputs(rng):
    T = rng.integers(-200, 201, (N, 8, 16, W)); R = T + rng.integers(-40, 41, T.shape); L = draw_lists(rng)
    share = rng.choice(np.array([1.0, 0.3, 0.02, 0.0]), (N, 8, N, F))
    return pack(R, frames(rng, T, L, share), L)
def setup_inputs_chain(rng):
    R = rng.integers(-200, 201, (N, 8, 16, W)); L = draw_lists(rng); B = np.zeros((N, 8, 16, N, F, K), np.int64)
    for q in range(N):
        for g in range(8):
            c = rng.permutation(W); P, Q = c[:K], c[K:2 * K]; R[q, g][:, Q] = R[q, g][:, P]
            away = rng.integers(1, 51, (16, K)) * (2 * rng.integers(0, 2, (16, K)) - 1)
            for r in range(N):
                for f in range(F):
                    z = rng.permutation(K); o = rng.permutation(O); e = 1 if rng.random() < 0.7 else -1
                    L[r, g, q, f, o[0]] = P[z]; L[r, g, q, f, o[1]] = Q[z]
                    B[r, g, :, q, f] = (R[q, g][:, P] + e * away)[:, z]
    return pack(R, B, L)
def setup_inputs_edges(rng):
    R = rng.integers(-200, 201, (N, 8, 16, W)); L = draw_lists(rng); B = np.zeros((N, 8, 16, N, F, K), np.int64)
    o = rng.integers(0, O, (N, 8, N, F)); same = rng.random((N, 8, N, F)) < 0.3
    for q in range(N):
        same[q, 0, q, 0] = True; same[q, 1, q, 0] = False
        for r in range(N):
            for f in range(F):
                s = rng.choice(np.array([0, 1, C - 1, C, C + 1, 2 * C]), (8, 16, K)) * (2 * rng.integers(0, 2, (8, 16, K)) - 1)
                B[r, :, :, q, f] = pick(R[q], L[r, np.arange(8), q, f, o[r, :, q, f]]) + np.where(same[r, :, q, f][:, None, None], 0, s)
    return pack(R, B, L)
def setup_inputs_ends(rng):
    R = rng.integers(10, V + 1, (N, 8, 16, W)); L = draw_lists(rng); B = rng.choice(np.array([-V, 1 - V, -1, 0, 1, V - 1, V]), (N, 8, 16, N, F, K))
    runs = [np.arange(K), np.arange(W - K, W), np.arange(K)[::-1], np.arange(W - 1, W - 1 - K, -1), np.arange(K) * (W // K)]
    z = rng.permuted(np.tile(np.arange(8), (N, 1)), axis=1)
    for q in range(N):
        for g in range(8):
            s = 2 * int(rng.integers(0, 2)) - 1; k = int(z[q, g])
            for r in range(N):
                for f in range(F):
                    for o in range(O):
                        i = int(rng.integers(0, len(runs) + 1))
                        L[r, g, q, f, o] = runs[i] if i < len(runs) else np.concatenate([[W - 1], 1 + rng.permutation(W - 2)[:K - 2], [0]])
            if k < 4: R[q, g] = rng.integers(V - 1 if k < 2 else 200, V + 1, (16, W))
            c = rng.permutation(W)
            for t in range(N * F if k % 2 == 1 else 1):
                r, f = (q + t // F) % N, t % F; p1, p2 = c[K - 1 + 2 * t], c[K + 2 * t]
                i = int(rng.integers(0, 16)); a = 259 + (k // 2) % 2 + 4 * int(rng.integers(0, 59)) - V
                R[q, g][:, p2] = R[q, g][:, p1]; R[q, g, i, p1] = a; R[q, g, i, p2] = a + 1
                near = np.append(c[:K - 1], p1); far = np.append(c[:K - 1], p2)
                w = int(rng.integers(1, O))
                if k == 0:
                    w = 1 + 3 * int(rng.integers(0, (O + 1) // 3))
                    if int(np.sum(R[q, g][:, near] + V)) % 2 == 1: R[q, g, 0, c[0]] = 2 * V - 1 - R[q, g, 0, c[0]]
                if k in (2, 3): w = 1 + 2 * int(rng.integers(0, O // 2))
                B[r, g, :, q, f] = -s * V
                for o in range(O): L[r, g, q, f, o] = rng.permutation(near if o == w else far)
            R[q, g] = s * R[q, g]
    return pack(R, B, L)
def setup_inputs_ties(rng):
    s = 2 * rng.integers(0, 2, (N, 8, 16, 1)) - 1; m = rng.integers(N * F * C - V, V - 2 * C, (N, 8, 16, 1))
    R = m + rng.integers(C, 2 * C + 1, (N, 8, 16, W)); R[..., W - 1] = V
    L = np.zeros((N, 8, N, F, O, K), np.int64); B = np.zeros((N, 8, 16, N, F, K), np.int64)
    for q in range(N):
        for g in range(8):
            S = rng.permutation(W - 1)[:K]
            for t in range(N * F):
                r, f = (q + t // F) % N, t % F
                if rng.random() < 0.5: S = rng.permutation(W - 1)[:K]
                w = int(rng.integers(0, O))
                for o in range(O):
                    p = rng.permutation(S)
                    if o < w or (o > w and rng.random() < 0.5): p[rng.integers(0, K)] = W - 1
                    L[r, g, q, f, o] = p
                B[r, g, :, q, f] = s[q, g] * (m[q, g] - t * C + rng.integers(0, C + 1, (16, K)))
    return pack(R * s, B, L)
def setup_inputs_spread(rng):
    z = np.exp2(-rng.integers(0, 9, (N, 8, 1, W)).astype(np.float64))
    T = (rng.integers(-V, V + 1, (N, 8, 16, W)) * z).astype(np.int64); R = np.clip(T + (rng.integers(-60, 61, T.shape) * z).astype(np.int64), -V, V); L = draw_lists(rng)
    share = rng.choice(np.array([1.0, 0.6, 0.1, 0.02, 0.0]), (N, 8, N, F))
    return pack(R, frames(rng, T, L, share), L)
def check_inputs(d):
    bad = []
    for k in ("ref0", "obs"):
        v = np.asarray(d[k]).astype(np.float32)
        if not (np.all(np.abs(v) <= V) and np.all(v == np.rint(v))): bad.append("range of " + k)
    if np.min(d["ops"]) < 0 or np.max(d["ops"]) > W - 1: bad.append("range of ops")
    for a in d["ops"]:
        e = np.sort(gentries(a).reshape(8, -1, K), axis=-1)
        if np.any(e[..., 1:] == e[..., :-1]):
            bad.append("repeated number in a list of ops"); break
    return bad
def reference(ref0, obs, ops):
    R = ref0.astype(np.float32).astype(np.int32).reshape(N, 8, 16, W); x = obs.astype(np.float32).astype(np.int32).reshape(N, 8, 16, N, F, K)
    L = np.stack([gentries(a) for a in ops]).astype(np.int64).reshape(N, 8, N, F, O, K)
    g, i = np.arange(8)[:, None, None], np.arange(16)[None, :, None]
    for q in range(N):
        for d in range(N):
            r = (q + d) % N
            for f in range(F):
                b = x[r, :, :, q, f]
                cost = np.stack([np.sum(np.abs(b - pick(R[q], L[r, :, q, f, o])), axis=(1, 2)) for o in range(O)])
                win = np.argmin(cost, axis=0)
                ix = L[r, np.arange(8), q, f, win]
                v = pick(R[q], ix)
                R[q][g, i, ix[:, None, :]] = v + np.clip(b - v, -C, C)
    return {"y": R.reshape(N, 128, W).astype(np.float32).astype(BF)}

@@ -1,0 +1,289 @@
+import numpy as np
+from concourse.mybir import dt, AluOpType, AxisListType, ActivationFunctionType
+
+N, W, K, F, O, C = 4, 4096, 640, 2, 4, 8
+LC = K // 16
+FC = O * LC
+Y = 104
+KY = K - Y
+HC, A1 = 20, 12
+H1, HA = 16 * HC, 16 * (HC + A1)
+R = K - 512
+E = 128
+
+SCRATCH = {
+    "ref": ("sbuf", [128, W], "bfloat16"),
+    "obsb": ("sbuf", [128, N * F * K], "bfloat16"),
+    "opsb": ("sbuf", [128, N * F * FC], "int32"),
+    "lo1": ("sbuf", [128, F * K], "bfloat16"),
+    "lo2": ("sbuf", [128, F * K], "bfloat16"),
+    "lo3": ("sbuf", [128, F * K], "bfloat16"),
+    "ll1": ("sbuf", [128, F * FC], "int32"),
+    "ll2": ("sbuf", [128, F * FC], "int32"),
+    "ll3": ("sbuf", [128, F * FC], "int32"),
+    "offs": ("sbuf", [128, N * F * FC], "uint16"),
+    "d0": ("sbuf", [128, K], "float16"),
+    "d1": ("sbuf", [128, K], "float16"),
+    "vall": ("sbuf", [128, O * K], "bfloat16"),
+    "junk2": ("sbuf", [128, K], "float32"),
+    "junk3": ("sbuf", [128, KY], "float32"),
+    "acc": ("sbuf", [128, 8], "float32"),
+    "accb": ("sbuf", [128, 8], "float32"),
+    "nmax": ("sbuf", [128, 8], "float32"),
+    "flag": ("sbuf", [128, 8], "float32"),
+    "wcol": ("sbuf", [128, 8], "float32"),
+    "low": ("sbuf", [128, 8], "float32"),
+    "sel": ("sbuf", [128, 16], "uint16"),
+    "selv": ("sbuf", [128, 48], "uint16"),
+    "offw": ("sbuf", [128, 48], "uint16"),
+    "dw": ("sbuf", [128, H1], "bfloat16"),
+    "vw": ("sbuf", [128, K], "bfloat16"),
+    "ew": ("sbuf", [128, K], "bfloat16"),
+    "onesf": ("sbuf", [128, 128], "float32"),
+    "blk0": ("sbuf", [128, 128], "float32"),
+    "blk": ("sbuf", [128, 128], "float32"),
+    "onesb": ("sbuf", [128, 128], "bfloat16"),
+    "negb": ("sbuf", [128, 128], "bfloat16"),
+    "eye": ("sbuf", [128, 128], "bfloat16"),
+    "neye": ("sbuf", [128, 128], "bfloat16"),
+    "neyeh": ("sbuf", [128, 128], "float16"),
+    "ip": ("sbuf", [128, LC], "int32"),
+    "ia": ("sbuf", [128, LC], "int32"),
+    "ic": ("sbuf", [128, LC], "int32"),
+    "bs": ("sbuf", [128, LC], "float32"),
+    "bt": ("sbuf", [128, 4], "float32"),
+    "base": ("sbuf", [128, 4], "float32"),
+    "basev": ("sbuf", [128, LC], "float32"),
+    "psa": ("psum", [128, 1024], "float32"),
+    "psb": ("psum", [128, 1024], "float32"),
+    "psc": ("psum", [128, 512], "float32"),
+    "psd": ("psum", [128, 512], "float32"),
+    "psf": ("psum", [128, 512], "float32"),
+    "psg": ("psum", [128, 512], "float32"),
+}
+SEMAPHORES = ["cv", "cs", "cp", "cg", "lops0", "lops1", "lobs0", "lobs1", "lref", "lsend1", "lsend2", "lsend3",
+              "llist1", "llist2", "llist3", "arr1", "arr2", "arr3", "sent", "yst"]
+
+
+def rank_program(g, core, T, topo):
+    q = T.rank_of(core)
+    if q is None:
+        return
+    A, X, FN = AluOpType, AxisListType, ActivationFunctionType
+    queue = {"v": g.vector, "s": g.scalar, "p": g.tensor, "g": g}
+    count = {"cv": 0, "cs": 0, "cp": 0, "cg": 0}
+    seen = {"v": {}, "s": {}, "p": {}, "g": {}}
+
+    def need(e, deps):
+        top = {}
+        for name, n in deps:
+            top[name] = max(top.get(name, 0), n)
+        for name in top:
+            if seen[e].get(name, 0) < top[name]:
+                queue[e].wait_ge(T.sem[name], top[name])
+                seen[e][name] = top[name]
+
+    def done(e, inst):
+        name = "c" + e
+        inst.then_inc(T.sem[name], 1)
+        count[name] += 1
+        return (name, count[name])
+
+    oc, bc = q * F * FC, q * F * K
+    g.sync.dma_start(T.opsb[:, oc:oc + FC], T.ops[:, oc:oc + FC]).then_inc(T.sem.lops0, 16)
+    g.scalar.dma_start(T.obsb[:, bc:bc + K], T.obs[:, bc:bc + K]).then_inc(T.sem.lobs0, 16)
+    g.sync.dma_start(T.ref[:], T.ref0[:]).then_inc(T.sem.lref, 16)
+
+    def load(d):
+        o = (q - d) % N
+        g.sync.dma_start(T.opsb[:, o * F * FC:(o + 1) * F * FC],
+                         T.ops[:, o * F * FC:(o + 1) * F * FC]).then_inc(T.sem["llist%d" % d], 16)
+        g.sync.dma_start(T.obsb[:, o * F * K:(o + 1) * F * K],
+                         T.obs[:, o * F * K:(o + 1) * F * K]).then_inc(T.sem["lsend%d" % d], 16)
+
+    load(1)
+    g.sync.dma_start(T.opsb[:, oc + FC:oc + 2 * FC], T.ops[:, oc + FC:oc + 2 * FC]).then_inc(T.sem.lops1, 16)
+    g.sync.dma_start(T.obsb[:, bc + K:bc + 2 * K], T.obs[:, bc + K:bc + 2 * K]).then_inc(T.sem.lobs1, 16)
+    load(2)
+    load(3)
+
+    m1 = done("v", g.vector.memset(T.onesb[:], 1.0))
+    m2 = done("v", g.vector.memset(T.negb[:], -1.0))
+    m3 = done("v", g.vector.memset(T.onesf[:], -1.0))
+    done("v", g.vector.memset(T.low[:], -1.0e9))
+    mz = done("v", g.vector.memset(T.accb[:], 0.0))
+    i1 = done("g", g.iota(T.ip[:], [[16, LC]], 0, 1))
+    i2 = done("g", g.iota(T.ic[:], [[16, LC]], 0, 0))
+    need("g", [m1])
+    te = done("g", g.affine_select(T.eye[:], T.onesb[:], [[-1, 128]], A.is_equal, 0.0, 0, 1))
+    need("g", [m2])
+    tn = done("g", g.affine_select(T.neye[:], T.negb[:], [[-1, 128]], A.is_equal, 0.0, 0, 1))
+    need("g", [m3])
+    b0 = done("g", g.affine_select(T.blk0[:], T.onesf[:], [[-16, 8], [0, 16]], A.is_ge, 0.0, 0, 1))
+    need("g", [b0])
+    tb = done("g", g.affine_select(T.blk[:], T.blk0[:], [[16, 8], [0, 16]], A.is_ge, 0.0, 15, -1))
+    need("v", [i1])
+    k1 = done("v", g.vector.tensor_scalar(T.ia[:], T.ip[:], 15, None, A.bitwise_and))
+    need("v", [k1, i2])
+    k2 = done("v", g.vector.tensor_tensor(T.bs[:], T.ia[:], T.ic[:], A.add))
+    need("v", [k2])
+    k3 = done("v", g.vector.tensor_scalar(T.bt[:], T.bs[:, 0:4], float(LC - 1), 0.25, A.min, A.add))
+    kbv = done("v", g.vector.tensor_scalar(T.basev[:], T.bs[:], 0.25, 1.0 / K, A.add, A.mult))
+    need("v", [k3])
+    kbase = done("v", g.vector.tensor_scalar(T.base[:], T.bt[:], 1.0 / LC, None, A.mult))
+    need("v", [tn])
+    th = done("v", g.vector.tensor_copy(T.neyeh[:], T.neye[:]))
+
+    nsent = 0
+    for d in range(1, N):
+        o = (q - d) % N
+        dst = T.cores[o]
+        rid, pid, _ = topo.addr(dst)
+        mask = topo.mask(core, dst)
+        ne = len(topo.engines(core, dst))
+        for land, src, sem in ((T["ll%d" % d], T.opsb[:, o * F * FC:(o + 1) * F * FC], T.sem["llist%d" % d]),
+                               (T["lo%d" % d], T.obsb[:, o * F * K:(o + 1) * F * K], T.sem["lsend%d" % d])):
+            g.wait_ge(sem, 16)
+            g.remote_dma(land[:], src, T.sem["arr%d" % d], T.sem.sent, pid, rid, mask)
+            nsent += ne
+
+    def frame(t):
+        d, f = t // F, t % F
+        if d == 0:
+            b = T.obsb
+            c0 = bc + f * K
+            dep = [("lobs%d" % f, 16)]
+            ldep = [("lops%d" % f, 16)]
+            lw = T.opsb[:, oc + f * FC:oc + (f + 1) * FC]
+        else:
+            b = T["lo%d" % d]
+            c0 = f * K
+            src = T.cores[(q + d) % N]
+            dep = ldep = [("arr%d" % d, 2 * len(topo.engines(src, core)))]
+            lw = T["ll%d" % d][:, f * FC:(f + 1) * FC]
+        return b, c0, dep, lw, ldep
+
+    def convert(t):
+        _, _, _, lw, ldep = frame(t)
+        need("v", ldep)
+        return done("v", g.vector.tensor_copy(T.offs[:, t * FC:(t + 1) * FC], lw))
+
+    def mm(out, lhsT, rhs, start, stop):
+        return done("p", g.tensor.matmul(out, lhsT[:], rhs, start, stop))
+
+    psy = T.psc[:, 128:128 + Y]
+
+    def lay(t, free_a, free_b, free_d, free_f):
+        b, c0, dep, _, _ = frame(t)
+        need("p", dep + free_a)
+        mm(T.psa[:, 0:512], T.eye, b[:, c0:c0 + 512], True, False)
+        mm(T.psa[:, 512:K], T.eye, b[:, c0 + 512:c0 + K], True, False)
+        need("p", free_d)
+        mm(T.psd[:, 0:512], T.neye, b[:, c0:c0 + 512], True, False)
+        need("p", free_b)
+        mm(T.psb[:, 0:512], T.eye, b[:, c0:c0 + 512], True, False)
+        mm(T.psb[:, 512:KY], T.eye, b[:, c0 + 512:c0 + KY], True, False)
+        mm(psy, T.eye, b[:, c0 + KY:c0 + K], True, False)
+        need("p", free_f)
+        mm(T.psf[:, 0:512], T.neye, b[:, c0:c0 + 512], True, False)
+
+    def values(o, ps, d, b, c0):
+        mm(ps[:, 0:512], T.neyeh, d[:, 0:512], False, True)
+        rest = T.psg[:, o * R:(o + 1) * R]
+        mm(rest, T.neye, b[:, c0 + 512:c0 + K], True, False)
+        return mm(rest, T.neyeh, d[:, 512:K], False, True)
+
+    conv = {0: convert(0)}
+    need("p", [te, tn])
+    lay(0, [], [], [], [])
+    need("p", [tb, mz, th])
+
+    ready = [("lref", 16)]
+    win = T.ref[:, 0:W]
+    vwin = T.vall[:, 0:O * K]
+    NT = N * F
+    for t in range(NT):
+        b, c0, dep, lw, _ = frame(t)
+        off = lambda a: T.offs[:, t * FC + a * LC:t * FC + (a + 1) * LC]
+        val = lambda a: T.vall[:, a * K:(a + 1) * K]
+        need("v", ready + dep + [conv[t]])
+        g0 = done("v", g.vector.tensor_tensor(T.d0[:], win.indirect(off(0)), b[:, c0:c0 + K], A.subtract))
+        g1 = done("v", g.vector.tensor_tensor(T.d1[:], win.indirect(off(1)), b[:, c0:c0 + K], A.subtract))
+        need("s", ready + [conv[t]])
+        g2 = done("s", g.scalar.activation(val(2), win.indirect(off(2)), FN.Identity, scale=-1.0))
+        g3 = done("s", g.scalar.activation(val(3), win.indirect(off(3)), FN.Identity, scale=-1.0))
+        need("p", [g2])
+        mm(T.psa[:, 0:512], T.eye, T.vall[:, 2 * K:2 * K + 512], False, True)
+        w2 = mm(T.psa[:, 512:K], T.eye, T.vall[:, 2 * K + 512:3 * K], False, True)
+        need("p", [g0])
+        v0 = values(0, T.psd, T.d0, b, c0)
+        need("p", [g3])
+        wy = mm(psy, T.eye, T.vall[:, 3 * K + KY:4 * K], False, True)
+        mm(T.psb[:, 0:512], T.eye, T.vall[:, 3 * K:3 * K + 512], False, True)
+        w3 = mm(T.psb[:, 512:KY], T.eye, T.vall[:, 3 * K + 512:3 * K + KY], False, True)
+        need("p", [g1])
+        v1 = values(1, T.psf, T.d1, b, c0)
+        need("v", [g0])
+        done("v", g.vector.tensor_reduce(T.acc[:, 0:1], T.d0[:], X.X, A.add, apply_absolute_value=True))
+        need("v", [wy])
+        ry = done("v", g.vector.tensor_reduce(T.accb[:, 3:4], psy, X.X, A.add, apply_absolute_value=True))
+        need("v", [g1])
+        r1 = done("v", g.vector.tensor_reduce(T.acc[:, 1:2], T.d1[:], X.X, A.add, apply_absolute_value=True))
+        need("s", [w2])
+        a2 = done("s", g.scalar.activation(T.junk2[:], T.psa[:, 0:K], FN.Abs, accum_out=T.acc[:, 2:3]))
+        need("s", [w3])
+        a3 = done("s", g.scalar.activation(T.junk3[:], T.psb[:, 0:KY], FN.Abs, accum_out=T.acc[:, 3:4]))
+        need("s", [v0])
+        cs = done("s", g.scalar.activation(T.vall[:, 0:512], T.psd[:, 0:512], FN.Identity))
+        need("p", [ry])
+        mm(T.psc[:, 0:O], T.blk, T.accb[:, 0:O], True, False)
+        need("p", [r1, a3])
+        el = mm(T.psc[:, 0:O], T.blk, T.acc[:, 0:O], False, True)
+        need("v", [v1])
+        done("v", g.vector.tensor_copy(T.vall[:, 512:K], T.psg[:, 0:R]))
+        done("v", g.vector.tensor_copy(T.vall[:, K + 512:2 * K], T.psg[:, R:2 * R]))
+        done("v", g.vector.tensor_copy(T.vall[:, K:K + E], T.psf[:, 0:E]))
+        need("v", [el])
+        e1 = done("v", g.vector.tensor_tensor_scan(T.nmax[:, 0:O], T.psc[:, 0:O], T.low[:, 0:O], -1.0e9, A.max, A.max))
+        cv = done("v", g.vector.tensor_copy(T.vall[:, K + E:K + 512], T.psf[:, E:512]))
+        need("s", [e1])
+        e3 = done("s", g.scalar.activation(T.flag[:, 0:O - 1], T.nmax[:, 0:O - 1], FN.Sign, bias=T.nmax[:, O - 1:O], scale=-1.0,
+                                           accum_out=T.wcol[:, 0:1]))
+        need("p", [cs])
+        mm(T.psd[:, 0:HA - H1], T.eye, b[:, c0 + H1:c0 + HA], True, False)
+        need("p", [cv])
+        mm(T.psf[:, 0:K - HA], T.eye, b[:, c0 + HA:c0 + K], True, False)
+        need("v", [e3, kbase, kbv])
+        e4 = done("v", g.vector.tensor_scalar(T.selv[:, 0:LC], T.basev[:], T.wcol[:, 0:1], float(K), A.add, A.mult))
+        e5 = done("v", g.vector.tensor_scalar(T.sel[:, 0:3], T.base[:, 0:3], T.wcol[:, 0:1], float(LC), A.add, A.mult))
+        need("v", [e4, cs])
+        x1 = done("v", g.vector.tensor_tensor(T.dw[:], vwin.indirect(T.selv[:, 0:HC]), b[:, c0:c0 + H1], A.add))
+        need("v", [e5])
+        e6 = done("v", g.vector.tensor_copy(T.offw[:, 0:48], lw.indirect(T.sel[:, 0:3])))
+        need("s", [e4])
+        s2 = done("s", g.scalar.activation(T.vw[:, H1:HA], vwin.indirect(T.selv[:, HC:HC + A1]), FN.Identity, scale=-1.0))
+        s3 = done("s", g.scalar.activation(T.vw[:, HA:K], vwin.indirect(T.selv[:, HC + A1:LC]), FN.Identity, scale=-1.0))
+        s1 = done("s", g.scalar.activation(T.vw[:, 0:H1], vwin.indirect(T.selv[:, 0:HC]), FN.Identity, scale=-1.0))
+        need("p", [s2])
+        x2 = mm(T.psd[:, 0:HA - H1], T.neye, T.vw[:, H1:HA], False, True)
+        need("p", [s3])
+        x3 = mm(T.psf[:, 0:K - HA], T.neye, T.vw[:, HA:K], False, True)
+        need("v", [x1])
+        y1 = done("v", g.vector.tensor_scalar(T.ew[:, 0:H1], T.dw[:], float(C), float(-C), A.min, A.max))
+        need("v", [x2])
+        y2 = done("v", g.vector.tensor_scalar(T.ew[:, H1:HA], T.psd[:, 0:HA - H1], float(C), float(-C), A.min, A.max))
+        need("v", [x3])
+        y3 = done("v", g.vector.tensor_scalar(T.ew[:, HA:K], T.psf[:, 0:K - HA], float(C), float(-C), A.min, A.max))
+        if t < NT - 1:
+            conv[t + 1] = convert(t + 1)
+        need("v", [e6, y1, y2, y3, s1])
+        sc = done("v", g.vector.tensor_tensor(win.indirect(T.offw[:, 0:LC]), T.vw[:], T.ew[:], A.add))
+        ready = [sc]
+        if t < NT - 1:
+            lay(t + 1, [a2], [a3, e1], [y2], [y3])
+
+    g.sync.wait_ge(T.sem.cv, count["cv"])
+    g.sync.dma_start(T.y[:], T.ref[:]).then_inc(T.sem.yst, 16)
+    g.sync.wait_ge(T.sem.yst, 16)
+    g.wait_ge(T.sem.sent, nsent)
+    need("g", [(c, count[c]) for c in ("cv", "cs", "cp", "cg")])

@@ -4,12 +4,17 @@ from concourse.mybir import dt, AluOpType, AxisListType, ActivationFunctionType
 N, W, K, F, O, C = 4, 4096, 640, 2, 4, 8
 LC = K // 16
 FC = O * LC
-Y = 104
+Y = 64
 KY = K - Y
-HC, A1 = 20, 12
-H1, HA = 16 * HC, 16 * (HC + A1)
-R = K - 512
-E = 128
+IL = True
+SP = 128
+COST = ["ry", "r0x", "r1", "a2", "w0", "w3z", "w3a", "lv", "v1v", "v1s", "a3z", "a3a", "r0", "e0", "ee", "el"]
+LATE = ["a2", "a3", "a3a", "r0", "r1"]
+JV = 128
+MID = -5.0 * 2 ** 21
+NC = O
+PIECES = [(256, "D"), (192, "V"), (192, "P")]
+AFTER = ["d2v", "d1v", "d3s", "cs", "d0s", "e1", "e2", "cv", "l2", "e4", "s2", "sa", "e6", "x1", "x0", "y1", "y2", "conv", "sc2"]
 
 SCRATCH = {
     "ref": ("sbuf", [128, W], "bfloat16"),
@@ -22,21 +27,26 @@ SCRATCH = {
     "ll2": ("sbuf", [128, F * FC], "int32"),
     "ll3": ("sbuf", [128, F * FC], "int32"),
     "offs": ("sbuf", [128, N * F * FC], "uint16"),
-    "d0": ("sbuf", [128, K], "float16"),
     "d1": ("sbuf", [128, K], "float16"),
     "vall": ("sbuf", [128, O * K], "bfloat16"),
+    "dall": ("sbuf", [128, O * K], "bfloat16"),
     "junk2": ("sbuf", [128, K], "float32"),
-    "junk3": ("sbuf", [128, KY], "float32"),
-    "acc": ("sbuf", [128, 8], "float32"),
-    "accb": ("sbuf", [128, 8], "float32"),
-    "nmax": ("sbuf", [128, 8], "float32"),
-    "flag": ("sbuf", [128, 8], "float32"),
+    "junk3": ("sbuf", [128, K], "float32"),
+    "m1": ("sbuf", [128, K], "float16"),
+    "acc": ("sbuf", [128, 16], "float32"),
+    "accb": ("sbuf", [128, 16], "float32"),
+    "nmin": ("sbuf", [128, 16], "float32"),
+    "nlow": ("sbuf", [128, 8], "float32"),
     "wcol": ("sbuf", [128, 8], "float32"),
-    "low": ("sbuf", [128, 8], "float32"),
+    "step": ("sbuf", [128, 16], "float32"),
+    "mid": ("sbuf", [128, 16], "bfloat16"),
+    "grp": ("sbuf", [128, 8], "float16"),
+    "part": ("sbuf", [128, 8], "float32"),
     "sel": ("sbuf", [128, 16], "uint16"),
     "selv": ("sbuf", [128, 48], "uint16"),
     "offw": ("sbuf", [128, 48], "uint16"),
-    "dw": ("sbuf", [128, H1], "bfloat16"),
+    "dw": ("sbuf", [128, K], "bfloat16"),
+    "uw": ("sbuf", [128, K], "bfloat16"),
     "vw": ("sbuf", [128, K], "bfloat16"),
     "ew": ("sbuf", [128, K], "bfloat16"),
     "onesf": ("sbuf", [128, 128], "float32"),
@@ -53,16 +63,17 @@ SCRATCH = {
     "bs": ("sbuf", [128, LC], "float32"),
     "bt": ("sbuf", [128, 4], "float32"),
     "base": ("sbuf", [128, 4], "float32"),
-    "basev": ("sbuf", [128, LC], "float32"),
+    "basev": ("sbuf", [128, LC + 4], "float32"),
+    "lf": ("sbuf", [128, FC], "float32"),
+    "li": ("sbuf", [128, FC], "float32"),
     "psa": ("psum", [128, 1024], "float32"),
     "psb": ("psum", [128, 1024], "float32"),
-    "psc": ("psum", [128, 512], "float32"),
-    "psd": ("psum", [128, 512], "float32"),
+    "psy": ("psum", [128, 512], "float32"),
+    "psc": ("psum", [128, 1024], "float32"),
     "psf": ("psum", [128, 512], "float32"),
-    "psg": ("psum", [128, 512], "float32"),
 }
-SEMAPHORES = ["cv", "cs", "cp", "cg", "lops0", "lops1", "lobs0", "lobs1", "lref", "lsend1", "lsend2", "lsend3",
-              "llist1", "llist2", "llist3", "arr1", "arr2", "arr3", "sent", "yst"]
+SEMAPHORES = ["cv", "cs", "cp", "cg", "lops0", "lops1", "lobs0", "lobs1", "lref", "lsend1", "lsend1b", "lsend2", "lsend3",
+              "llist1", "llist2", "llist3", "arr1", "arr1b", "arr2", "arr3", "sent", "sent1", "yst"]
 
 
 def rank_program(g, core, T, topo):
@@ -91,26 +102,39 @@ def rank_program(g, core, T, topo):
 
     oc, bc = q * F * FC, q * F * K
     g.sync.dma_start(T.opsb[:, oc:oc + FC], T.ops[:, oc:oc + FC]).then_inc(T.sem.lops0, 16)
-    g.scalar.dma_start(T.obsb[:, bc:bc + K], T.obs[:, bc:bc + K]).then_inc(T.sem.lobs0, 16)
     g.sync.dma_start(T.ref[:], T.ref0[:]).then_inc(T.sem.lref, 16)
+    g.sync.dma_start(T.obsb[:, bc:bc + K], T.obs[:, bc:bc + K]).then_inc(T.sem.lobs0, 16)
 
-    def load(d):
+    def goods(d):
         o = (q - d) % N
-        g.sync.dma_start(T.opsb[:, o * F * FC:(o + 1) * F * FC],
-                         T.ops[:, o * F * FC:(o + 1) * F * FC]).then_inc(T.sem["llist%d" % d], 16)
-        g.sync.dma_start(T.obsb[:, o * F * K:(o + 1) * F * K],
-                         T.obs[:, o * F * K:(o + 1) * F * K]).then_inc(T.sem["lsend%d" % d], 16)
+        l0, b0 = o * F * FC, o * F * K
+        out = [("llist%d" % d, T["ll%d" % d][:], T.opsb[:, l0:l0 + F * FC], T.ops[:, l0:l0 + F * FC], "arr%d" % d)]
+        if d == 1:
+            out.append(("lsend1", T.lo1[:, 0:K], T.obsb[:, b0:b0 + K], T.obs[:, b0:b0 + K], "arr1"))
+            out.append(("lsend1b", T.lo1[:, K:2 * K], T.obsb[:, b0 + K:b0 + 2 * K], T.obs[:, b0 + K:b0 + 2 * K], "arr1b"))
+        else:
+            out.append(("lsend%d" % d, T["lo%d" % d][:], T.obsb[:, b0:b0 + F * K], T.obs[:, b0:b0 + F * K], "arr%d" % d))
+        return out
 
-    load(1)
+    def load(items):
+        for name, _, here, there, _ in items:
+            g.sync.dma_start(here, there).then_inc(T.sem[name], 16)
+
+    load(goods(1)[0:2])
     g.sync.dma_start(T.opsb[:, oc + FC:oc + 2 * FC], T.ops[:, oc + FC:oc + 2 * FC]).then_inc(T.sem.lops1, 16)
     g.sync.dma_start(T.obsb[:, bc + K:bc + 2 * K], T.obs[:, bc + K:bc + 2 * K]).then_inc(T.sem.lobs1, 16)
-    load(2)
-    load(3)
+    load(goods(1)[2:])
+    g.sync.wait_ge(T.sem.sent1, 2 * len(topo.engines(core, T.cores[(q - 1) % N])))
+    load(goods(2))
+    load(goods(3))
 
     m1 = done("v", g.vector.memset(T.onesb[:], 1.0))
     m2 = done("v", g.vector.memset(T.negb[:], -1.0))
-    m3 = done("v", g.vector.memset(T.onesf[:], -1.0))
-    done("v", g.vector.memset(T.low[:], -1.0e9))
+    m3 = done("v", g.vector.memset(T.onesf[:], 4.0))
+    done("v", g.vector.memset(T.step[:, 0:O - 1], 1.0))
+    done("v", g.vector.memset(T.step[:, O - 1:O], 0.0))
+    done("v", g.vector.memset(T.mid[:], MID))
+    done("v", g.vector.memset(T.acc[:], 0.0))
     mz = done("v", g.vector.memset(T.accb[:], 0.0))
     i1 = done("g", g.iota(T.ip[:], [[16, LC]], 0, 1))
     i2 = done("g", g.iota(T.ic[:], [[16, LC]], 0, 0))
@@ -128,24 +152,22 @@ def rank_program(g, core, T, topo):
     k2 = done("v", g.vector.tensor_tensor(T.bs[:], T.ia[:], T.ic[:], A.add))
     need("v", [k2])
     k3 = done("v", g.vector.tensor_scalar(T.bt[:], T.bs[:, 0:4], float(LC - 1), 0.25, A.min, A.add))
-    kbv = done("v", g.vector.tensor_scalar(T.basev[:], T.bs[:], 0.25, 1.0 / K, A.add, A.mult))
+    done("v", g.vector.tensor_scalar(T.basev[:, LC:LC + 4], T.bs[:, 0:4], float(LC - 1), float(O), A.min, A.mult))
+    kbv = done("v", g.vector.tensor_scalar(T.basev[:, 0:LC], T.bs[:], float(O), None, A.mult))
     need("v", [k3])
     kbase = done("v", g.vector.tensor_scalar(T.base[:], T.bt[:], 1.0 / LC, None, A.mult))
     need("v", [tn])
     th = done("v", g.vector.tensor_copy(T.neyeh[:], T.neye[:]))
 
-    nsent = 0
-    for d in range(1, N):
-        o = (q - d) % N
-        dst = T.cores[o]
+    nsent = [0]
+
+    def send(d):
+        dst = T.cores[(q - d) % N]
         rid, pid, _ = topo.addr(dst)
-        mask = topo.mask(core, dst)
-        ne = len(topo.engines(core, dst))
-        for land, src, sem in ((T["ll%d" % d], T.opsb[:, o * F * FC:(o + 1) * F * FC], T.sem["llist%d" % d]),
-                               (T["lo%d" % d], T.obsb[:, o * F * K:(o + 1) * F * K], T.sem["lsend%d" % d])):
-            g.wait_ge(sem, 16)
-            g.remote_dma(land[:], src, T.sem["arr%d" % d], T.sem.sent, pid, rid, mask)
-            nsent += ne
+        for name, land, here, _, arr in goods(d):
+            g.wait_ge(T.sem[name], 16)
+            g.remote_dma(land, here, T.sem[arr], T.sem.sent1 if arr == "arr1" else T.sem.sent, pid, rid, topo.mask(core, dst))
+            nsent[0] += 0 if arr == "arr1" else len(topo.engines(core, dst))
 
     def frame(t):
         d, f = t // F, t % F
@@ -158,8 +180,10 @@ def rank_program(g, core, T, topo):
         else:
             b = T["lo%d" % d]
             c0 = f * K
-            src = T.cores[(q + d) % N]
-            dep = ldep = [("arr%d" % d, 2 * len(topo.engines(src, core)))]
+            ne = len(topo.engines(T.cores[(q + d) % N], core))
+            dep = ldep = [("arr%d" % d, 2 * ne)]
+            if d == 1 and f == 1:
+                dep = [("arr1b", ne)]
             lw = T["ll%d" % d][:, f * FC:(f + 1) * FC]
         return b, c0, dep, lw, ldep
 
@@ -168,122 +192,232 @@ def rank_program(g, core, T, topo):
         need("v", ldep)
         return done("v", g.vector.tensor_copy(T.offs[:, t * FC:(t + 1) * FC], lw))
 
+    def weave(t):
+        _, _, _, lw, ldep = frame(t)
+        need("v", ldep)
+        need("g", [done("v", g.vector.tensor_copy(T.lf[:], lw))])
+        for o in range(O):
+            last = done("g", g.affine_select(T.li[:, o:FC:O], T.lf[:, o * LC:(o + 1) * LC], [[0, LC]], A.is_ge, 0.0, 0, 0))
+        return last
+
     def mm(out, lhsT, rhs, start, stop):
         return done("p", g.tensor.matmul(out, lhsT[:], rhs, start, stop))
 
-    psy = T.psc[:, 128:128 + Y]
+    def val(o, j0, j1):
+        return T.vall[:, O * j0 + o:O * j1:O]
 
-    def lay(t, free_a, free_b, free_d, free_f):
+    def lay(t, free, banks="abcfwxyz"):
         b, c0, dep, _, _ = frame(t)
-        need("p", dep + free_a)
-        mm(T.psa[:, 0:512], T.eye, b[:, c0:c0 + 512], True, False)
-        mm(T.psa[:, 512:K], T.eye, b[:, c0 + 512:c0 + K], True, False)
-        need("p", free_d)
-        mm(T.psd[:, 0:512], T.neye, b[:, c0:c0 + 512], True, False)
-        need("p", free_b)
-        mm(T.psb[:, 0:512], T.eye, b[:, c0:c0 + 512], True, False)
-        mm(T.psb[:, 512:KY], T.eye, b[:, c0 + 512:c0 + KY], True, False)
-        mm(psy, T.eye, b[:, c0 + KY:c0 + K], True, False)
-        need("p", free_f)
-        mm(T.psf[:, 0:512], T.neye, b[:, c0:c0 + 512], True, False)
+        need("p", dep)
+        for bank, sign, j0, j1 in (("b", T.eye, 0, min(KY, 512)), ("w", T.eye, 512, KY), ("c", T.eye, 0, 512), ("y", T.eye, KY, K),
+                                   ("x", T.eye, 512, K), ("a", T.eye, 0, 512), ("f", T.neye, JV, K), ("z", T.eye, 512, K)):
+            need("p", free[bank] if free else [])
+            if j1 > j0 and bank in banks:
+                mm(room(bank, j1 - j0), sign, b[:, c0 + j0:c0 + j1], True, False)
 
-    def values(o, ps, d, b, c0):
-        mm(ps[:, 0:512], T.neyeh, d[:, 0:512], False, True)
-        rest = T.psg[:, o * R:(o + 1) * R]
-        mm(rest, T.neye, b[:, c0 + 512:c0 + K], True, False)
-        return mm(rest, T.neyeh, d[:, 512:K], False, True)
+    def room(bank, n):
+        return {"w": T.psb, "x": T.psc, "z": T.psa}[bank][:, 512:512 + n] if bank in "wxz" else T["ps" + bank][:, 0:n]
 
+    costs = T.psb[:, 1020:1024]
+    junk = {"a2": T.junk2[:, 0:KY], "a3": T.junk3[:], "a3a": T.junk3[:, 0:512], "a3z": T.junk3[:, 512:K]}
     conv = {0: convert(0)}
     need("p", [te, tn])
-    lay(0, [], [], [], [])
+    lay(0, None, "bwyx")
     need("p", [tb, mz, th])
 
+    starts = [sum(n for n, _ in PIECES[:k]) for k in range(len(PIECES) + 1)]
+    pull_ps = ["x", "y", "z", "a"]
     ready = [("lref", 16)]
     win = T.ref[:, 0:W]
-    vwin = T.vall[:, 0:O * K]
     NT = N * F
     for t in range(NT):
         b, c0, dep, lw, _ = frame(t)
         off = lambda a: T.offs[:, t * FC + a * LC:t * FC + (a + 1) * LC]
-        val = lambda a: T.vall[:, a * K:(a + 1) * K]
-        need("v", ready + dep + [conv[t]])
-        g0 = done("v", g.vector.tensor_tensor(T.d0[:], win.indirect(off(0)), b[:, c0:c0 + K], A.subtract))
+        if IL:
+            woven = weave(t)
+        if t < N - 1:
+            send(t + 1)
+        need("v", ready + [conv[t]])
+        g0 = done("v", g.vector.tensor_scalar(val(0, 0, K), win.indirect(off(0)), -1.0, None, A.mult))
+        need("v", dep)
         g1 = done("v", g.vector.tensor_tensor(T.d1[:], win.indirect(off(1)), b[:, c0:c0 + K], A.subtract))
         need("s", ready + [conv[t]])
-        g2 = done("s", g.scalar.activation(val(2), win.indirect(off(2)), FN.Identity, scale=-1.0))
-        g3 = done("s", g.scalar.activation(val(3), win.indirect(off(3)), FN.Identity, scale=-1.0))
+        g2 = done("s", g.scalar.activation(val(2, 0, K), win.indirect(off(2)), FN.Identity, scale=-1.0))
+        g3 = done("s", g.scalar.activation(val(3, 0, K), win.indirect(off(3)), FN.Identity, scale=-1.0))
         need("p", [g2])
-        mm(T.psa[:, 0:512], T.eye, T.vall[:, 2 * K:2 * K + 512], False, True)
-        w2 = mm(T.psa[:, 512:K], T.eye, T.vall[:, 2 * K + 512:3 * K], False, True)
+        y2 = mm(T.psy[:, 0:Y], T.eye, val(2, KY, K), False, True)
         need("p", [g0])
-        v0 = values(0, T.psd, T.d0, b, c0)
-        need("p", [g3])
-        wy = mm(psy, T.eye, T.vall[:, 3 * K + KY:4 * K], False, True)
-        mm(T.psb[:, 0:512], T.eye, T.vall[:, 3 * K:3 * K + 512], False, True)
-        w3 = mm(T.psb[:, 512:KY], T.eye, T.vall[:, 3 * K + 512:3 * K + KY], False, True)
-        need("p", [g1])
-        v1 = values(1, T.psf, T.d1, b, c0)
-        need("v", [g0])
-        done("v", g.vector.tensor_reduce(T.acc[:, 0:1], T.d0[:], X.X, A.add, apply_absolute_value=True))
-        need("v", [wy])
-        ry = done("v", g.vector.tensor_reduce(T.accb[:, 3:4], psy, X.X, A.add, apply_absolute_value=True))
-        need("v", [g1])
-        r1 = done("v", g.vector.tensor_reduce(T.acc[:, 1:2], T.d1[:], X.X, A.add, apply_absolute_value=True))
-        need("s", [w2])
-        a2 = done("s", g.scalar.activation(T.junk2[:], T.psa[:, 0:K], FN.Abs, accum_out=T.acc[:, 2:3]))
-        need("s", [w3])
-        a3 = done("s", g.scalar.activation(T.junk3[:], T.psb[:, 0:KY], FN.Abs, accum_out=T.acc[:, 3:4]))
-        need("s", [v0])
-        cs = done("s", g.scalar.activation(T.vall[:, 0:512], T.psd[:, 0:512], FN.Identity))
-        need("p", [ry])
-        mm(T.psc[:, 0:O], T.blk, T.accb[:, 0:O], True, False)
-        need("p", [r1, a3])
-        el = mm(T.psc[:, 0:O], T.blk, T.acc[:, 0:O], False, True)
-        need("v", [v1])
-        done("v", g.vector.tensor_copy(T.vall[:, 512:K], T.psg[:, 0:R]))
-        done("v", g.vector.tensor_copy(T.vall[:, K + 512:2 * K], T.psg[:, R:2 * R]))
-        done("v", g.vector.tensor_copy(T.vall[:, K:K + E], T.psf[:, 0:E]))
-        need("v", [el])
-        e1 = done("v", g.vector.tensor_tensor_scan(T.nmax[:, 0:O], T.psc[:, 0:O], T.low[:, 0:O], -1.0e9, A.max, A.max))
-        cv = done("v", g.vector.tensor_copy(T.vall[:, K + E:K + 512], T.psf[:, E:512]))
-        need("s", [e1])
-        e3 = done("s", g.scalar.activation(T.flag[:, 0:O - 1], T.nmax[:, 0:O - 1], FN.Sign, bias=T.nmax[:, O - 1:O], scale=-1.0,
-                                           accum_out=T.wcol[:, 0:1]))
-        need("p", [cs])
-        mm(T.psd[:, 0:HA - H1], T.eye, b[:, c0 + H1:c0 + HA], True, False)
-        need("p", [cv])
-        mm(T.psf[:, 0:K - HA], T.eye, b[:, c0 + HA:c0 + K], True, False)
-        need("v", [e3, kbase, kbv])
-        e4 = done("v", g.vector.tensor_scalar(T.selv[:, 0:LC], T.basev[:], T.wcol[:, 0:1], float(K), A.add, A.mult))
-        e5 = done("v", g.vector.tensor_scalar(T.sel[:, 0:3], T.base[:, 0:3], T.wcol[:, 0:1], float(LC), A.add, A.mult))
-        need("v", [e4, cs])
-        x1 = done("v", g.vector.tensor_tensor(T.dw[:], vwin.indirect(T.selv[:, 0:HC]), b[:, c0:c0 + H1], A.add))
-        need("v", [e5])
-        e6 = done("v", g.vector.tensor_copy(T.offw[:, 0:48], lw.indirect(T.sel[:, 0:3])))
-        need("s", [e4])
-        s2 = done("s", g.scalar.activation(T.vw[:, H1:HA], vwin.indirect(T.selv[:, HC:HC + A1]), FN.Identity, scale=-1.0))
-        s3 = done("s", g.scalar.activation(T.vw[:, HA:K], vwin.indirect(T.selv[:, HC + A1:LC]), FN.Identity, scale=-1.0))
-        s1 = done("s", g.scalar.activation(T.vw[:, 0:H1], vwin.indirect(T.selv[:, 0:HC]), FN.Identity, scale=-1.0))
-        need("p", [s2])
-        x2 = mm(T.psd[:, 0:HA - H1], T.neye, T.vw[:, H1:HA], False, True)
-        need("p", [s3])
-        x3 = mm(T.psf[:, 0:K - HA], T.neye, T.vw[:, HA:K], False, True)
-        need("v", [x1])
-        y1 = done("v", g.vector.tensor_scalar(T.ew[:, 0:H1], T.dw[:], float(C), float(-C), A.min, A.max))
-        need("v", [x2])
-        y2 = done("v", g.vector.tensor_scalar(T.ew[:, H1:HA], T.psd[:, 0:HA - H1], float(C), float(-C), A.min, A.max))
-        need("v", [x3])
-        y3 = done("v", g.vector.tensor_scalar(T.ew[:, HA:K], T.psf[:, 0:K - HA], float(C), float(-C), A.min, A.max))
+        x0 = mm(T.psc[:, 512:K], T.eye, val(0, 512, K), False, True)
+        w2 = mm(T.psb[:, 0:min(KY, 512)], T.eye, val(2, 0, min(KY, 512)), False, True)
+        if KY > 512:
+            w2 = mm(T.psb[:, 512:KY], T.eye, val(2, 512, KY), False, True)
+        if t == 0:
+            lay(0, None, "cafz")
+        c = {}
+        parts = {"r0": ("v", "w0", T.psc[:, 0:512], 3), "r0x": ("v", x0, T.psc[:, 512:K], 3), "r1": ("v", g1, T.d1[:], 2),
+                 "ry": ("v", y2, T.psy[:, 0:Y], 1), "a2": ("s", w2, T.psb[:, 0:KY], 1),
+                 "a3": ("s", "w3a", T.psa[:, 0:K], 0), "a3a": ("s", "w3a", T.psa[:, 0:512], 0), "a3z": ("s", "w3z", T.psa[:, 512:K], 0)}
+        last_e = [x for x in COST if x[0] == "e"][-1]
+        for name in COST:
+            if name in parts:
+                e, dp, src, col = parts[name]
+                out = (T.acc if name in LATE else T.accb)[:, col:col + 1]
+                need(e, [c[dp], c["w3z"]] if e == "s" and name != "a2" and name != "a3z" else [c.get(dp, dp)])
+                if e == "v":
+                    c[name] = done("v", g.vector.tensor_reduce(out, src, X.X, A.add, apply_absolute_value=True))
+                else:
+                    c[name] = done("s", g.scalar.activation(junk[name], src, FN.Abs, accum_out=out))
+            elif name == "w0":
+                c[name] = mm(T.psc[:, 0:512], T.eye, val(0, 0, 512), False, True)
+            elif name == "w3a":
+                need("p", [g3])
+                c[name] = mm(T.psa[:, 0:512], T.eye, val(3, 0, 512), False, True)
+            elif name == "w3z":
+                need("p", [g3])
+                c[name] = mm(T.psa[:, 512:K], T.eye, val(3, 512, K), False, True)
+            elif name == "lv":
+                need("p", [c["ry"]])
+                mm(T.psy[:, 0:JV], T.neye, b[:, c0:c0 + JV], True, False)
+                c[name] = 1
+            elif name == "v1v":
+                need("p", [g1] * c["lv"])
+                v1v = mm(T.psy[:, 0:JV], T.neyeh, T.d1[:, 0:JV], False, True)
+            elif name == "v1s":
+                need("p", [g1])
+                v1s = mm(T.psf[:, 0:K - JV], T.neyeh, T.d1[:, JV:K], False, True)
+            elif name == "e0":
+                need("p", [c["a2"]])
+                mm(costs, T.eye, T.mid[:, 0:O], True, False)
+                c[name] = 1
+            else:
+                need("p", [c[x] for x in COST if x in parts and (x in LATE) == (name == "el")] * c["e0"])
+                el = mm(costs, T.blk, (T.acc if name == "el" else T.accb)[:, 0:O], False, name == last_e)
+        free = {"a": [c.get("a3") or c["a3a"]], "z": [c.get("a3") or c["a3z"]], "c": [c["r0"]], "x": [c["r0x"]], "b": [c["a2"]]}
+        bank = {}
+        for k in range(len(PIECES)):
+            if PIECES[k][1] not in "VD":
+                bank[k] = pull_ps[len(bank)]
+
+        r = {}
+        ND = PIECES[0][0] if PIECES[0][1] == "D" else 0
+
+        def vwin(buf, k):
+            copies = [r["cv"]] if starts[k + 1] <= JV else [r["cv"], r["cs"]]
+            return buf[:, 0:O * starts[k + 1]].indirect(T.selv[:, starts[k] // 16:starts[k + 1] // 16]), copies
+
+        def copy(e, out, in_):
+            if e == "v":
+                return done("v", g.vector.tensor_copy(out, in_))
+            return done("s", g.scalar.activation(out, in_, FN.Identity))
+
+        for name in AFTER:
+            kind, k = name, None
+            if name[-1].isdigit() and name[:-1] in ("x", "s", "y", "c", "u", "v", "sc", "l"):
+                kind, k = name[:-1], int(name[-1])
+                j0, j1 = starts[k], starts[k + 1]
+                mode = PIECES[k][1]
+                ps = room(bank[k], j1 - j0) if k in bank else None
+            if kind == "cv":
+                need("v", [v1v])
+                r[name] = copy("v", val(1, 0, JV), T.psy[:, 0:JV])
+                free["y"] = [r[name]]
+            elif kind == "cs":
+                need("s", [v1s])
+                r[name] = copy("s", val(1, JV, K), T.psf[:, 0:K - JV])
+                free["f"] = [r[name]]
+            elif kind[0] == "d":
+                o, e = int(kind[1]), kind[2]
+                j0, j1 = {"": (0, ND), "a": (0, SP), "b": (SP, ND)}[kind[3:]]
+                out = T.dall[:, O * j0 + o:O * j1:O]
+                if o == 1:
+                    r[name] = done("v", g.vector.tensor_scalar(out, T.d1[:, j0:j1], -1.0, None, A.mult))
+                else:
+                    bk = {0: "c", 2: "b", 3: "a"}[o]
+                    need(e, [x for x in free[bk] if x[0] != "c" + e])
+                    r[name] = copy(e, out, T["ps" + bk][:, j0:j1])
+                    free[bk] = [r[name]]
+            elif kind == "l":
+                need("p", free[bank[k]])
+                r[name] = mm(ps, T.eye, b[:, c0 + j0:c0 + j1], True, False)
+            elif kind == "e1":
+                need("v", [el])
+                r[name] = done("v", g.vector.tensor_tensor_scan(T.nmin[:, 0:NC], costs, T.step[:, 0:NC], 1.0e9, A.min, A.add))
+            elif kind == "e2":
+                r[name] = done("v", g.vector.tensor_reduce(T.nlow[:, 0:1], costs, X.X, A.min, negate=True))
+                free["w"] = [r["e1"], r[name]]
+            elif kind == "conv":
+                if t < NT - 1:
+                    conv[t + 1] = convert(t + 1)
+            elif kind == "e4":
+                need("v", [r["e1"], r["e2"], kbv])
+                r[name] = done("v", g.vector.tensor_scalar(T.selv[:, 0:LC + 4], T.basev[:], T.nmin[:, NC - 1:NC], T.nlow[:, 0:1], A.add, A.add))
+            elif kind == "wq":
+                need("s", [r["e1"], r["e2"]])
+                r["wq"] = done("s", g.scalar.activation(T.wcol[:, 0:1], T.nmin[:, NC - 1:NC], FN.Identity, bias=T.nlow[:, 0:1]))
+            elif kind == "wv":
+                need("v", [r["e1"], r["e2"]])
+                r["wq"] = done("v", g.vector.tensor_scalar(T.wcol[:, 0:1], T.nmin[:, NC - 1:NC], T.nlow[:, 0:1], None, A.add))
+            elif kind == "e5":
+                need("v", [r["wq"], kbase])
+                r[name] = done("v", g.vector.tensor_scalar(T.sel[:, 0:3], T.base[:, 0:3], T.wcol[:, 0:1], float(LC), A.add, A.mult))
+            elif kind == "e6" and IL:
+                need("v", [r["e4"], woven])
+                r[name] = done("v", g.vector.tensor_copy(T.offw[:, 0:48], T.li[:, 0:FC].indirect(T.selv[:, LC:LC + 3])))
+            elif kind == "e6":
+                need("v", [r["e5"]])
+                r[name] = done("v", g.vector.tensor_copy(T.offw[:, 0:48], lw.indirect(T.sel[:, 0:3])))
+            elif kind == "x" and mode == "D":
+                w, _ = vwin(T.dall, k)
+                need("v", [r["e4"]] + [r[x] for x in AFTER if x[0] == "d"])
+                r["y%d" % k] = done("v", g.vector.tensor_scalar(T.ew[:, j0:j1], w, float(C), float(-C), A.min, A.max))
+            elif kind == "x":
+                w, copies = vwin(T.vall, k)
+                need("v", [r["e4"]] + copies)
+                r[name] = done("v", g.vector.tensor_tensor(T.dw[:, j0:j1], w, b[:, c0 + j0:c0 + j1], A.add))
+            elif kind == "sa":
+                w, copies = vwin(T.vall, 1)
+                w = T.vall[:, 0:O * starts[2]].indirect(T.selv[:, 0:starts[2] // 16])
+                need("s", [r["e4"]] + copies)
+                r["s0"] = r["s1"] = done("s", g.scalar.activation(T.vw[:, 0:starts[2]], w, FN.Identity, scale=-1.0))
+            elif kind == "s":
+                w, copies = vwin(T.vall, k)
+                need("s", [r["e4"]] + copies)
+                r[name] = done("s", g.scalar.activation(T.vw[:, j0:j1], w, FN.Identity, scale=-1.0))
+                if k in bank:
+                    need("p", [r[name]] if r["l%d" % k] else [])
+                    r["p%d" % k] = mm(ps, T.neye, T.vw[:, j0:j1], False, True)
+            elif kind == "c":
+                need("s", [r["p%d" % k]])
+                if mode == "C":
+                    r["x%d" % k] = done("s", g.scalar.activation(T.dw[:, j0:j1], ps, FN.Identity))
+                    free[bank[k]] = [r["x%d" % k]]
+                else:
+                    r[name] = done("s", g.scalar.activation(T.dw[:, j0:j1], ps, FN.Relu, bias=float(C)))
+                    free[bank[k]] = [r[name]]
+            elif kind == "u":
+                need("s", [r["c%d" % k]])
+                r[name] = done("s", g.scalar.activation(T.uw[:, j0:j1], T.dw[:, j0:j1], FN.Relu, bias=float(2 * C), scale=-1.0))
+            elif kind == "v":
+                need("s", [r["u%d" % k]])
+                r["y%d" % k] = done("s", g.scalar.activation(T.ew[:, j0:j1], T.uw[:, j0:j1], FN.Identity, bias=float(C), scale=-1.0))
+            elif kind == "y":
+                src = ps if mode == "P" else T.dw[:, j0:j1]
+                need("v", [r[("p%d" if mode == "P" else "x%d") % k]])
+                r[name] = done("v", g.vector.tensor_scalar(T.ew[:, j0:j1], src, float(C), float(-C), A.min, A.max))
+                if mode == "P":
+                    free[bank[k]] = [r[name]]
+            elif kind == "sc":
+                k0 = r.get("scattered", 0)
+                j0 = starts[k0]
+                need("v", ready + [r["e6"]] + [r[n % i] for i in range(k0, k + 1) for n in ("y%d", "s%d")])
+                r[name] = done("v", g.vector.tensor_tensor(win.indirect(T.offw[:, j0 // 16:j1 // 16]), T.vw[:, j0:j1], T.ew[:, j0:j1], A.add))
+                r["scattered"] = k + 1
+                ready = [r[name]]
         if t < NT - 1:
-            conv[t + 1] = convert(t + 1)
-        need("v", [e6, y1, y2, y3, s1])
-        sc = done("v", g.vector.tensor_tensor(win.indirect(T.offw[:, 0:LC]), T.vw[:], T.ew[:], A.add))
-        ready = [sc]
-        if t < NT - 1:
-            lay(t + 1, [a2], [a3, e1], [y2], [y3])
+            lay(t + 1, free)
 
     g.sync.wait_ge(T.sem.cv, count["cv"])
     g.sync.dma_start(T.y[:], T.ref[:]).then_inc(T.sem.yst, 16)
     g.sync.wait_ge(T.sem.yst, 16)
-    g.wait_ge(T.sem.sent, nsent)
+    g.wait_ge(T.sem.sent, nsent[0])
     need("g", [(c, count[c]) for c in ("cv", "cs", "cp", "cg")])

import numpy as np
from concourse.mybir import dt, AluOpType, AxisListType, ActivationFunctionType

N, W, K, F, O, C = 4, 4096, 640, 2, 4, 8
LC = K // 16
FC = O * LC
Y = 64
KY = K - Y
IL = True
SP = 128
COST = ["ry", "r0x", "r1", "a2", "w0", "w3z", "w3a", "lv", "v1v", "v1s", "a3z", "a3a", "r0", "e0", "ee", "el"]
LATE = ["a2", "a3", "a3a", "r0", "r1"]
JV = 128
MID = -5.0 * 2 ** 21
NC = O
PIECES = [(256, "D"), (192, "V"), (192, "P")]
AFTER = ["d2v", "d1v", "d3s", "cs", "d0s", "e1", "e2", "cv", "l2", "e4", "s2", "sa", "e6", "x1", "x0", "y1", "y2", "conv", "sc2"]

SCRATCH = {
    "ref": ("sbuf", [128, W], "bfloat16"),
    "obsb": ("sbuf", [128, N * F * K], "bfloat16"),
    "opsb": ("sbuf", [128, N * F * FC], "int32"),
    "lo1": ("sbuf", [128, F * K], "bfloat16"),
    "lo2": ("sbuf", [128, F * K], "bfloat16"),
    "lo3": ("sbuf", [128, F * K], "bfloat16"),
    "ll1": ("sbuf", [128, F * FC], "int32"),
    "ll2": ("sbuf", [128, F * FC], "int32"),
    "ll3": ("sbuf", [128, F * FC], "int32"),
    "offs": ("sbuf", [128, N * F * FC], "uint16"),
    "d1": ("sbuf", [128, K], "float16"),
    "vall": ("sbuf", [128, O * K], "bfloat16"),
    "dall": ("sbuf", [128, O * K], "bfloat16"),
    "junk2": ("sbuf", [128, K], "float32"),
    "junk3": ("sbuf", [128, K], "float32"),
    "m1": ("sbuf", [128, K], "float16"),
    "acc": ("sbuf", [128, 16], "float32"),
    "accb": ("sbuf", [128, 16], "float32"),
    "nmin": ("sbuf", [128, 16], "float32"),
    "nlow": ("sbuf", [128, 8], "float32"),
    "wcol": ("sbuf", [128, 8], "float32"),
    "step": ("sbuf", [128, 16], "float32"),
    "mid": ("sbuf", [128, 16], "bfloat16"),
    "grp": ("sbuf", [128, 8], "float16"),
    "part": ("sbuf", [128, 8], "float32"),
    "sel": ("sbuf", [128, 16], "uint16"),
    "selv": ("sbuf", [128, 48], "uint16"),
    "offw": ("sbuf", [128, 48], "uint16"),
    "dw": ("sbuf", [128, K], "bfloat16"),
    "uw": ("sbuf", [128, K], "bfloat16"),
    "vw": ("sbuf", [128, K], "bfloat16"),
    "ew": ("sbuf", [128, K], "bfloat16"),
    "onesf": ("sbuf", [128, 128], "float32"),
    "blk0": ("sbuf", [128, 128], "float32"),
    "blk": ("sbuf", [128, 128], "float32"),
    "onesb": ("sbuf", [128, 128], "bfloat16"),
    "negb": ("sbuf", [128, 128], "bfloat16"),
    "eye": ("sbuf", [128, 128], "bfloat16"),
    "neye": ("sbuf", [128, 128], "bfloat16"),
    "neyeh": ("sbuf", [128, 128], "float16"),
    "ip": ("sbuf", [128, LC], "int32"),
    "ia": ("sbuf", [128, LC], "int32"),
    "ic": ("sbuf", [128, LC], "int32"),
    "bs": ("sbuf", [128, LC], "float32"),
    "bt": ("sbuf", [128, 4], "float32"),
    "base": ("sbuf", [128, 4], "float32"),
    "basev": ("sbuf", [128, LC + 4], "float32"),
    "lf": ("sbuf", [128, FC], "float32"),
    "li": ("sbuf", [128, FC], "float32"),
    "psa": ("psum", [128, 1024], "float32"),
    "psb": ("psum", [128, 1024], "float32"),
    "psy": ("psum", [128, 512], "float32"),
    "psc": ("psum", [128, 1024], "float32"),
    "psf": ("psum", [128, 512], "float32"),
}
SEMAPHORES = ["cv", "cs", "cp", "cg", "lops0", "lops1", "lobs0", "lobs1", "lref", "lsend1", "lsend1b", "lsend2", "lsend3",
              "llist1", "llist2", "llist3", "arr1", "arr1b", "arr2", "arr3", "sent", "sent1", "yst"]


def rank_program(g, core, T, topo):
    q = T.rank_of(core)
    if q is None:
        return
    A, X, FN = AluOpType, AxisListType, ActivationFunctionType
    queue = {"v": g.vector, "s": g.scalar, "p": g.tensor, "g": g}
    count = {"cv": 0, "cs": 0, "cp": 0, "cg": 0}
    seen = {"v": {}, "s": {}, "p": {}, "g": {}}

    def need(e, deps):
        top = {}
        for name, n in deps:
            top[name] = max(top.get(name, 0), n)
        for name in top:
            if seen[e].get(name, 0) < top[name]:
                queue[e].wait_ge(T.sem[name], top[name])
                seen[e][name] = top[name]

    def done(e, inst):
        name = "c" + e
        inst.then_inc(T.sem[name], 1)
        count[name] += 1
        return (name, count[name])

    oc, bc = q * F * FC, q * F * K
    g.sync.dma_start(T.opsb[:, oc:oc + FC], T.ops[:, oc:oc + FC]).then_inc(T.sem.lops0, 16)
    g.sync.dma_start(T.ref[:], T.ref0[:]).then_inc(T.sem.lref, 16)
    g.sync.dma_start(T.obsb[:, bc:bc + K], T.obs[:, bc:bc + K]).then_inc(T.sem.lobs0, 16)

    def goods(d):
        o = (q - d) % N
        l0, b0 = o * F * FC, o * F * K
        out = [("llist%d" % d, T["ll%d" % d][:], T.opsb[:, l0:l0 + F * FC], T.ops[:, l0:l0 + F * FC], "arr%d" % d)]
        if d == 1:
            out.append(("lsend1", T.lo1[:, 0:K], T.obsb[:, b0:b0 + K], T.obs[:, b0:b0 + K], "arr1"))
            out.append(("lsend1b", T.lo1[:, K:2 * K], T.obsb[:, b0 + K:b0 + 2 * K], T.obs[:, b0 + K:b0 + 2 * K], "arr1b"))
        else:
            out.append(("lsend%d" % d, T["lo%d" % d][:], T.obsb[:, b0:b0 + F * K], T.obs[:, b0:b0 + F * K], "arr%d" % d))
        return out

    def load(items):
        for name, _, here, there, _ in items:
            g.sync.dma_start(here, there).then_inc(T.sem[name], 16)

    load(goods(1)[0:2])
    g.sync.dma_start(T.opsb[:, oc + FC:oc + 2 * FC], T.ops[:, oc + FC:oc + 2 * FC]).then_inc(T.sem.lops1, 16)
    g.sync.dma_start(T.obsb[:, bc + K:bc + 2 * K], T.obs[:, bc + K:bc + 2 * K]).then_inc(T.sem.lobs1, 16)
    load(goods(1)[2:])
    g.sync.wait_ge(T.sem.sent1, 2 * len(topo.engines(core, T.cores[(q - 1) % N])))
    load(goods(2))
    load(goods(3))

    m1 = done("v", g.vector.memset(T.onesb[:], 1.0))
    m2 = done("v", g.vector.memset(T.negb[:], -1.0))
    m3 = done("v", g.vector.memset(T.onesf[:], 4.0))
    done("v", g.vector.memset(T.step[:, 0:O - 1], 1.0))
    done("v", g.vector.memset(T.step[:, O - 1:O], 0.0))
    done("v", g.vector.memset(T.mid[:], MID))
    done("v", g.vector.memset(T.acc[:], 0.0))
    mz = done("v", g.vector.memset(T.accb[:], 0.0))
    i1 = done("g", g.iota(T.ip[:], [[16, LC]], 0, 1))
    i2 = done("g", g.iota(T.ic[:], [[16, LC]], 0, 0))
    need("g", [m1])
    te = done("g", g.affine_select(T.eye[:], T.onesb[:], [[-1, 128]], A.is_equal, 0.0, 0, 1))
    need("g", [m2])
    tn = done("g", g.affine_select(T.neye[:], T.negb[:], [[-1, 128]], A.is_equal, 0.0, 0, 1))
    need("g", [m3])
    b0 = done("g", g.affine_select(T.blk0[:], T.onesf[:], [[-16, 8], [0, 16]], A.is_ge, 0.0, 0, 1))
    need("g", [b0])
    tb = done("g", g.affine_select(T.blk[:], T.blk0[:], [[16, 8], [0, 16]], A.is_ge, 0.0, 15, -1))
    need("v", [i1])
    k1 = done("v", g.vector.tensor_scalar(T.ia[:], T.ip[:], 15, None, A.bitwise_and))
    need("v", [k1, i2])
    k2 = done("v", g.vector.tensor_tensor(T.bs[:], T.ia[:], T.ic[:], A.add))
    need("v", [k2])
    k3 = done("v", g.vector.tensor_scalar(T.bt[:], T.bs[:, 0:4], float(LC - 1), 0.25, A.min, A.add))
    done("v", g.vector.tensor_scalar(T.basev[:, LC:LC + 4], T.bs[:, 0:4], float(LC - 1), float(O), A.min, A.mult))
    kbv = done("v", g.vector.tensor_scalar(T.basev[:, 0:LC], T.bs[:], float(O), None, A.mult))
    need("v", [k3])
    kbase = done("v", g.vector.tensor_scalar(T.base[:], T.bt[:], 1.0 / LC, None, A.mult))
    need("v", [tn])
    th = done("v", g.vector.tensor_copy(T.neyeh[:], T.neye[:]))

    nsent = [0]

    def send(d):
        dst = T.cores[(q - d) % N]
        rid, pid, _ = topo.addr(dst)
        for name, land, here, _, arr in goods(d):
            g.wait_ge(T.sem[name], 16)
            g.remote_dma(land, here, T.sem[arr], T.sem.sent1 if arr == "arr1" else T.sem.sent, pid, rid, topo.mask(core, dst))
            nsent[0] += 0 if arr == "arr1" else len(topo.engines(core, dst))

    def frame(t):
        d, f = t // F, t % F
        if d == 0:
            b = T.obsb
            c0 = bc + f * K
            dep = [("lobs%d" % f, 16)]
            ldep = [("lops%d" % f, 16)]
            lw = T.opsb[:, oc + f * FC:oc + (f + 1) * FC]
        else:
            b = T["lo%d" % d]
            c0 = f * K
            ne = len(topo.engines(T.cores[(q + d) % N], core))
            dep = ldep = [("arr%d" % d, 2 * ne)]
            if d == 1 and f == 1:
                dep = [("arr1b", ne)]
            lw = T["ll%d" % d][:, f * FC:(f + 1) * FC]
        return b, c0, dep, lw, ldep

    def convert(t):
        _, _, _, lw, ldep = frame(t)
        need("v", ldep)
        return done("v", g.vector.tensor_copy(T.offs[:, t * FC:(t + 1) * FC], lw))

    def weave(t):
        _, _, _, lw, ldep = frame(t)
        need("v", ldep)
        need("g", [done("v", g.vector.tensor_copy(T.lf[:], lw))])
        for o in range(O):
            last = done("g", g.affine_select(T.li[:, o:FC:O], T.lf[:, o * LC:(o + 1) * LC], [[0, LC]], A.is_ge, 0.0, 0, 0))
        return last

    def mm(out, lhsT, rhs, start, stop):
        return done("p", g.tensor.matmul(out, lhsT[:], rhs, start, stop))

    def val(o, j0, j1):
        return T.vall[:, O * j0 + o:O * j1:O]

    def lay(t, free, banks="abcfwxyz"):
        b, c0, dep, _, _ = frame(t)
        need("p", dep)
        for bank, sign, j0, j1 in (("b", T.eye, 0, min(KY, 512)), ("w", T.eye, 512, KY), ("c", T.eye, 0, 512), ("y", T.eye, KY, K),
                                   ("x", T.eye, 512, K), ("a", T.eye, 0, 512), ("f", T.neye, JV, K), ("z", T.eye, 512, K)):
            need("p", free[bank] if free else [])
            if j1 > j0 and bank in banks:
                mm(room(bank, j1 - j0), sign, b[:, c0 + j0:c0 + j1], True, False)

    def room(bank, n):
        return {"w": T.psb, "x": T.psc, "z": T.psa}[bank][:, 512:512 + n] if bank in "wxz" else T["ps" + bank][:, 0:n]

    costs = T.psb[:, 1020:1024]
    junk = {"a2": T.junk2[:, 0:KY], "a3": T.junk3[:], "a3a": T.junk3[:, 0:512], "a3z": T.junk3[:, 512:K]}
    conv = {0: convert(0)}
    need("p", [te, tn])
    lay(0, None, "bwyx")
    need("p", [tb, mz, th])

    starts = [sum(n for n, _ in PIECES[:k]) for k in range(len(PIECES) + 1)]
    pull_ps = ["x", "y", "z", "a"]
    ready = [("lref", 16)]
    win = T.ref[:, 0:W]
    NT = N * F
    for t in range(NT):
        b, c0, dep, lw, _ = frame(t)
        off = lambda a: T.offs[:, t * FC + a * LC:t * FC + (a + 1) * LC]
        if IL:
            woven = weave(t)
        if t < N - 1:
            send(t + 1)
        need("v", ready + [conv[t]])
        g0 = done("v", g.vector.tensor_scalar(val(0, 0, K), win.indirect(off(0)), -1.0, None, A.mult))
        need("v", dep)
        g1 = done("v", g.vector.tensor_tensor(T.d1[:], win.indirect(off(1)), b[:, c0:c0 + K], A.subtract))
        need("s", ready + [conv[t]])
        g2 = done("s", g.scalar.activation(val(2, 0, K), win.indirect(off(2)), FN.Identity, scale=-1.0))
        g3 = done("s", g.scalar.activation(val(3, 0, K), win.indirect(off(3)), FN.Identity, scale=-1.0))
        need("p", [g2])
        y2 = mm(T.psy[:, 0:Y], T.eye, val(2, KY, K), False, True)
        need("p", [g0])
        x0 = mm(T.psc[:, 512:K], T.eye, val(0, 512, K), False, True)
        w2 = mm(T.psb[:, 0:min(KY, 512)], T.eye, val(2, 0, min(KY, 512)), False, True)
        if KY > 512:
            w2 = mm(T.psb[:, 512:KY], T.eye, val(2, 512, KY), False, True)
        if t == 0:
            lay(0, None, "cafz")
        c = {}
        parts = {"r0": ("v", "w0", T.psc[:, 0:512], 3), "r0x": ("v", x0, T.psc[:, 512:K], 3), "r1": ("v", g1, T.d1[:], 2),
                 "ry": ("v", y2, T.psy[:, 0:Y], 1), "a2": ("s", w2, T.psb[:, 0:KY], 1),
                 "a3": ("s", "w3a", T.psa[:, 0:K], 0), "a3a": ("s", "w3a", T.psa[:, 0:512], 0), "a3z": ("s", "w3z", T.psa[:, 512:K], 0)}
        last_e = [x for x in COST if x[0] == "e"][-1]
        for name in COST:
            if name in parts:
                e, dp, src, col = parts[name]
                out = (T.acc if name in LATE else T.accb)[:, col:col + 1]
                need(e, [c[dp], c["w3z"]] if e == "s" and name != "a2" and name != "a3z" else [c.get(dp, dp)])
                if e == "v":
                    c[name] = done("v", g.vector.tensor_reduce(out, src, X.X, A.add, apply_absolute_value=True))
                else:
                    c[name] = done("s", g.scalar.activation(junk[name], src, FN.Abs, accum_out=out))
            elif name == "w0":
                c[name] = mm(T.psc[:, 0:512], T.eye, val(0, 0, 512), False, True)
            elif name == "w3a":
                need("p", [g3])
                c[name] = mm(T.psa[:, 0:512], T.eye, val(3, 0, 512), False, True)
            elif name == "w3z":
                need("p", [g3])
                c[name] = mm(T.psa[:, 512:K], T.eye, val(3, 512, K), False, True)
            elif name == "lv":
                need("p", [c["ry"]])
                mm(T.psy[:, 0:JV], T.neye, b[:, c0:c0 + JV], True, False)
                c[name] = 1
            elif name == "v1v":
                need("p", [g1] * c["lv"])
                v1v = mm(T.psy[:, 0:JV], T.neyeh, T.d1[:, 0:JV], False, True)
            elif name == "v1s":
                need("p", [g1])
                v1s = mm(T.psf[:, 0:K - JV], T.neyeh, T.d1[:, JV:K], False, True)
            elif name == "e0":
                need("p", [c["a2"]])
                mm(costs, T.eye, T.mid[:, 0:O], True, False)
                c[name] = 1
            else:
                need("p", [c[x] for x in COST if x in parts and (x in LATE) == (name == "el")] * c["e0"])
                el = mm(costs, T.blk, (T.acc if name == "el" else T.accb)[:, 0:O], False, name == last_e)
        free = {"a": [c.get("a3") or c["a3a"]], "z": [c.get("a3") or c["a3z"]], "c": [c["r0"]], "x": [c["r0x"]], "b": [c["a2"]]}
        bank = {}
        for k in range(len(PIECES)):
            if PIECES[k][1] not in "VD":
                bank[k] = pull_ps[len(bank)]

        r = {}
        ND = PIECES[0][0] if PIECES[0][1] == "D" else 0

        def vwin(buf, k):
            copies = [r["cv"]] if starts[k + 1] <= JV else [r["cv"], r["cs"]]
            return buf[:, 0:O * starts[k + 1]].indirect(T.selv[:, starts[k] // 16:starts[k + 1] // 16]), copies

        def copy(e, out, in_):
            if e == "v":
                return done("v", g.vector.tensor_copy(out, in_))
            return done("s", g.scalar.activation(out, in_, FN.Identity))

        for name in AFTER:
            kind, k = name, None
            if name[-1].isdigit() and name[:-1] in ("x", "s", "y", "c", "u", "v", "sc", "l"):
                kind, k = name[:-1], int(name[-1])
                j0, j1 = starts[k], starts[k + 1]
                mode = PIECES[k][1]
                ps = room(bank[k], j1 - j0) if k in bank else None
            if kind == "cv":
                need("v", [v1v])
                r[name] = copy("v", val(1, 0, JV), T.psy[:, 0:JV])
                free["y"] = [r[name]]
            elif kind == "cs":
                need("s", [v1s])
                r[name] = copy("s", val(1, JV, K), T.psf[:, 0:K - JV])
                free["f"] = [r[name]]
            elif kind[0] == "d":
                o, e = int(kind[1]), kind[2]
                j0, j1 = {"": (0, ND), "a": (0, SP), "b": (SP, ND)}[kind[3:]]
                out = T.dall[:, O * j0 + o:O * j1:O]
                if o == 1:
                    r[name] = done("v", g.vector.tensor_scalar(out, T.d1[:, j0:j1], -1.0, None, A.mult))
                else:
                    bk = {0: "c", 2: "b", 3: "a"}[o]
                    need(e, [x for x in free[bk] if x[0] != "c" + e])
                    r[name] = copy(e, out, T["ps" + bk][:, j0:j1])
                    free[bk] = [r[name]]
            elif kind == "l":
                need("p", free[bank[k]])
                r[name] = mm(ps, T.eye, b[:, c0 + j0:c0 + j1], True, False)
            elif kind == "e1":
                need("v", [el])
                r[name] = done("v", g.vector.tensor_tensor_scan(T.nmin[:, 0:NC], costs, T.step[:, 0:NC], 1.0e9, A.min, A.add))
            elif kind == "e2":
                r[name] = done("v", g.vector.tensor_reduce(T.nlow[:, 0:1], costs, X.X, A.min, negate=True))
                free["w"] = [r["e1"], r[name]]
            elif kind == "conv":
                if t < NT - 1:
                    conv[t + 1] = convert(t + 1)
            elif kind == "e4":
                need("v", [r["e1"], r["e2"], kbv])
                r[name] = done("v", g.vector.tensor_scalar(T.selv[:, 0:LC + 4], T.basev[:], T.nmin[:, NC - 1:NC], T.nlow[:, 0:1], A.add, A.add))
            elif kind == "wq":
                need("s", [r["e1"], r["e2"]])
                r["wq"] = done("s", g.scalar.activation(T.wcol[:, 0:1], T.nmin[:, NC - 1:NC], FN.Identity, bias=T.nlow[:, 0:1]))
            elif kind == "wv":
                need("v", [r["e1"], r["e2"]])
                r["wq"] = done("v", g.vector.tensor_scalar(T.wcol[:, 0:1], T.nmin[:, NC - 1:NC], T.nlow[:, 0:1], None, A.add))
            elif kind == "e5":
                need("v", [r["wq"], kbase])
                r[name] = done("v", g.vector.tensor_scalar(T.sel[:, 0:3], T.base[:, 0:3], T.wcol[:, 0:1], float(LC), A.add, A.mult))
            elif kind == "e6" and IL:
                need("v", [r["e4"], woven])
                r[name] = done("v", g.vector.tensor_copy(T.offw[:, 0:48], T.li[:, 0:FC].indirect(T.selv[:, LC:LC + 3])))
            elif kind == "e6":
                need("v", [r["e5"]])
                r[name] = done("v", g.vector.tensor_copy(T.offw[:, 0:48], lw.indirect(T.sel[:, 0:3])))
            elif kind == "x" and mode == "D":
                w, _ = vwin(T.dall, k)
                need("v", [r["e4"]] + [r[x] for x in AFTER if x[0] == "d"])
                r["y%d" % k] = done("v", g.vector.tensor_scalar(T.ew[:, j0:j1], w, float(C), float(-C), A.min, A.max))
            elif kind == "x":
                w, copies = vwin(T.vall, k)
                need("v", [r["e4"]] + copies)
                r[name] = done("v", g.vector.tensor_tensor(T.dw[:, j0:j1], w, b[:, c0 + j0:c0 + j1], A.add))
            elif kind == "sa":
                w, copies = vwin(T.vall, 1)
                w = T.vall[:, 0:O * starts[2]].indirect(T.selv[:, 0:starts[2] // 16])
                need("s", [r["e4"]] + copies)
                r["s0"] = r["s1"] = done("s", g.scalar.activation(T.vw[:, 0:starts[2]], w, FN.Identity, scale=-1.0))
            elif kind == "s":
                w, copies = vwin(T.vall, k)
                need("s", [r["e4"]] + copies)
                r[name] = done("s", g.scalar.activation(T.vw[:, j0:j1], w, FN.Identity, scale=-1.0))
                if k in bank:
                    need("p", [r[name]] if r["l%d" % k] else [])
                    r["p%d" % k] = mm(ps, T.neye, T.vw[:, j0:j1], False, True)
            elif kind == "c":
                need("s", [r["p%d" % k]])
                if mode == "C":
                    r["x%d" % k] = done("s", g.scalar.activation(T.dw[:, j0:j1], ps, FN.Identity))
                    free[bank[k]] = [r["x%d" % k]]
                else:
                    r[name] = done("s", g.scalar.activation(T.dw[:, j0:j1], ps, FN.Relu, bias=float(C)))
                    free[bank[k]] = [r[name]]
            elif kind == "u":
                need("s", [r["c%d" % k]])
                r[name] = done("s", g.scalar.activation(T.uw[:, j0:j1], T.dw[:, j0:j1], FN.Relu, bias=float(2 * C), scale=-1.0))
            elif kind == "v":
                need("s", [r["u%d" % k]])
                r["y%d" % k] = done("s", g.scalar.activation(T.ew[:, j0:j1], T.uw[:, j0:j1], FN.Identity, bias=float(C), scale=-1.0))
            elif kind == "y":
                src = ps if mode == "P" else T.dw[:, j0:j1]
                need("v", [r[("p%d" if mode == "P" else "x%d") % k]])
                r[name] = done("v", g.vector.tensor_scalar(T.ew[:, j0:j1], src, float(C), float(-C), A.min, A.max))
                if mode == "P":
                    free[bank[k]] = [r[name]]
            elif kind == "sc":
                k0 = r.get("scattered", 0)
                j0 = starts[k0]
                need("v", ready + [r["e6"]] + [r[n % i] for i in range(k0, k + 1) for n in ("y%d", "s%d")])
                r[name] = done("v", g.vector.tensor_tensor(win.indirect(T.offw[:, j0 // 16:j1 // 16]), T.vw[:, j0:j1], T.ew[:, j0:j1], A.add))
                r["scattered"] = k + 1
                ready = [r[name]]
        if t < NT - 1:
            lay(t + 1, free)

    g.sync.wait_ge(T.sem.cv, count["cv"])
    g.sync.dma_start(T.y[:], T.ref[:]).then_inc(T.sem.yst, 16)
    g.sync.wait_ge(T.sem.yst, 16)
    g.wait_ge(T.sem.sent, nsent[0])
    need("g", [(c, count[c]) for c in ("cv", "cs", "cp", "cg")])
